import numpy as np
CORES = [34,162,290,418,42,426]
N = 6
R, TK = 8, 512
def setup_inputs(rng):
    v = (rng.standard_normal((N, 128, R), dtype=np.float32) / np.float32(np.sqrt(128 * N)))
    return {"x": rng.standard_normal((N, 128, TK), dtype=np.float32), "v": v, "vt": v.transpose(0, 2, 1).copy()}
def setup_inputs_big(rng):
    d = setup_inputs(rng)
    for k in ("x",): d[k] = (d[k].astype(np.float32) * 1048576.0).astype(d[k].dtype)
    return d
def setup_inputs_small(rng):
    d = setup_inputs(rng)
    for k in ("x",): d[k] = (d[k].astype(np.float32) * (1 / 1048576.0)).astype(d[k].dtype)
    return d
def setup_inputs_apart(rng):
    d = setup_inputs(rng)
    f = (10.0 ** rng.permutation(np.linspace(-1.5, 1.5, N))).astype(np.float32).reshape(N, 1, 1)
    for k in ("x",): d[k] = (d[k].astype(np.float32) * f).astype(d[k].dtype)
    return d
def reference(x, v, vt):
    X, V, VT = x.astype(np.float64), v.astype(np.float64), vt.astype(np.float64)
    t = sum(V[j].T @ X[j] for j in range(N))
    return {"y": np.stack([X[r] - 2.0 * (VT[r].T @ t) for r in range(N)]).astype(np.float32)}

@@ -1,0 +1,196 @@
+from concourse.bass import DstId, RemoteDMATransfer
+from concourse.mybir import AluOpType
+
+P = 128
+TK = 512
+R = 8
+Q = 4
+B = 32
+WZ = B - R
+
+SCRATCH = {
+    "xs": ("sbuf", [P, TK], "float32"),
+    "ys": ("sbuf", [P, TK], "float32"),
+    "vr": ("sbuf", [P, R], "float32"),
+    "w": ("sbuf", [P, WZ + R + WZ], "float32"),
+    "z": ("sbuf", [P, Q * P], "float32"),
+    "own": ("sbuf", [P, B], "float32"),
+    "l1": ("sbuf", [P, B], "float32"),
+    "m2": ("sbuf", [P, 2 * B], "float32"),
+    "ta": ("sbuf", [P, P], "float32"),
+    "tb": ("sbuf", [P, P], "float32"),
+}
+for _i in range(Q):
+    SCRATCH["pp%d" % _i] = ("psum", [P, TK], "float32")
+    SCRATCH["py%d" % _i] = ("psum", [P, TK], "float32")
+
+SEMAPHORES = (["x0", "x1", "vl", "wz", "zz", "tz", "zl", "own", "a1", "a2", "snt", "sa", "sb", "s0", "s1"]
+              + ["pd%d" % i for i in range(Q)] + ["yd%d" % i for i in range(Q)] + ["yo%d" % i for i in range(Q)])
+
+
+def _links(topo, a, b):
+    if topo.host(a) == topo.host(b) and topo.chip(a) == topo.chip(b):
+        return 0
+    if topo.rack(topo.host(a)) == topo.rack(topo.host(b)):
+        return 1 if (topo.mates(a, b) or topo.same_plane(a, b)) else 2
+    return 1 if topo.chip(a) == topo.chip(b) else 3
+
+
+def _pairings(items):
+    if not items:
+        return [[]]
+    out = []
+    for i in range(1, len(items)):
+        for m in _pairings(items[1:i] + items[i + 1:]):
+            out.append([(items[0], items[i])] + m)
+    return out
+
+
+def _plan(cores, topo):
+    n = len(cores)
+    best = None
+    for m in _pairings(list(range(n))):
+        if not all(topo.may_write(cores[a], cores[b]) and topo.may_write(cores[b], cores[a]) for a, b in m):
+            continue
+        cost = sum(2 * _links(topo, cores[a], cores[b]) for a, b in m)
+        dests = [[] for _ in range(n)]
+        ok = True
+        for r in range(n):
+            for pair in m:
+                if r in pair:
+                    continue
+                cand = [s for s in pair if topo.may_write(cores[s], cores[r])]
+                if not cand:
+                    ok = False
+                    break
+                s = min(cand, key=lambda s: (_links(topo, cores[s], cores[r]), len(dests[s]), s))
+                dests[s].append(r)
+                cost += _links(topo, cores[s], cores[r])
+            if not ok:
+                break
+        if not ok:
+            continue
+        key = (max(len(d) for d in dests), cost)
+        if best is None or key < best[0]:
+            partner = [0] * n
+            for a, b in m:
+                partner[a], partner[b] = b, a
+            best = (key, partner, dests)
+    return best[1], best[2]
+
+
+def _count(mask):
+    return bin(mask).count("1")
+
+
+def rank_program(g, core, T, topo):
+    rank = T.rank_of(core)
+    if rank is None:
+        return
+    cores = list(T.cores)
+    partner, dests = _plan(cores, topo)
+    S = T.sem
+    pe, ve, sy, sc = g.tensor, g.vector, g.sync, g.scalar
+    H = TK // 2
+
+    def blk(q):
+        return slice(B * q, B * q + B)
+
+    sy.dma_start(T.xs[:, 0:H], T.x[:, 0:H]).then_inc(S.x0, 16)
+    sc.dma_start(T.vr[:], T.v[:]).then_inc(S.vl, 16)
+    sc.dma_start(T.xs[:, H:TK], T.x[:, H:TK]).then_inc(S.x1, 16)
+
+    ve.memset(T.w[:, 0:WZ], 0.0).then_inc(S.wz, 1)
+    ve.memset(T.w[:, WZ + R:WZ + R + WZ], 0.0).then_inc(S.wz, 1)
+    ve.memset(T.z[:], 0.0).then_inc(S.zz, 1)
+    ve.memset(T.ta[:], 0.0).then_inc(S.tz, 1)
+    ve.memset(T.tb[:], 0.0).then_inc(S.tz, 1)
+    ve.wait_ge(S.vl, 16)
+    ve.tensor_tensor(T.w[:, WZ:WZ + R], T.vr[:], T.vr[:], AluOpType.add).then_inc(S.wz, 1)
+
+    sy.wait_ge(S.zz, 1)
+    sc.wait_ge(S.zz, 1)
+    for q in range(Q):
+        for c in range(Q):
+            dq = sy if (q * Q + c) % 2 == 0 else sc
+            p0 = B * q + R * c
+            dq.dma_start(T.z[p0:p0 + R, P * c:P * c + P], T.vt[:]).then_inc(S.zl, 16)
+
+    pe.wait_ge(S.wz, 3)
+    pe.wait_ge(S.x0, 16)
+    for c in range(Q):
+        if c == Q // 2:
+            pe.wait_ge(S.x1, 16)
+        for q in range(Q):
+            col = (Q * c + q) * B
+            mm = pe.matmul(T["pp%d" % q][blk(q), 0:B], T.w[:, WZ - R * c:WZ - R * c + B], T.xs[:, col:col + B],
+                           start=(c == 0), stop=(c == Q - 1))
+            if c == Q - 1:
+                mm.then_inc(S["pd%d" % q], 1)
+
+    for q in range(Q):
+        ve.wait_ge(S["pd%d" % q], 1)
+        ve.tensor_copy(T.own[blk(q), :], T["pp%d" % q][blk(q), 0:B]).then_inc(S.own, 1)
+
+    pc = cores[partner[rank]]
+    m1 = topo.mask(core, pc)
+    rid, pid = topo.addr(pc, core)
+    g.wait_ge(S.own, Q)
+    g.remote_dma(out_ap=T.l1[:], in_ap=T.own[:], remote_sem=S.a1, local_sem=S.snt, pid=pid, routing_id=rid,
+                 dma_engine_mask=m1)
+    n_in1 = _count(topo.mask(pc, core))
+
+    def slot(dst, src):
+        return sorted(s for s in range(len(cores)) if dst in dests[s]).index(src)
+
+    def mask2(src):
+        m = -1
+        for d in dests[src]:
+            m &= topo.mask(cores[src], cores[d])
+        return m
+
+    g.wait_ge(S.a1, n_in1)
+    sent = _count(m1)
+    if dests[rank]:
+        ids, aps = [], []
+        for d in dests[rank]:
+            rid, pid = topo.addr(cores[d], core)
+            ids.append(DstId(rid=rid, pnc=pid))
+            k = slot(d, rank)
+            aps.append(T.m2[:, B * k:B * k + B])
+        g.remote_dma_fused([RemoteDMATransfer(dst_ids=ids, dma_engine_mask=mask2(rank), remote_sem=S.a2,
+                                              srcs=[T.own[:], T.l1[:]], dsts=aps, alu_op=1)], local_sem=S.snt)
+        sent += _count(mask2(rank))
+    n_in2 = sum(_count(mask2(s)) for s in range(len(cores)) if rank in dests[s])
+
+    ve.wait_ge(S.own, Q)
+    ve.wait_ge(S.tz, 2)
+    ve.wait_ge(S.a1, n_in1)
+    for q in range(Q):
+        ve.tensor_tensor(T.ta[blk(q), blk(q)], T.own[blk(q), :], T.l1[blk(q), :], AluOpType.add).then_inc(S.sa, 1)
+    pe.wait_ge(S.zl, 16 * Q * Q)
+    pe.wait_ge(S.sa, Q)
+    for c in range(Q):
+        pe.matmul(T["py%d" % c][:, 0:P], T.z[:, P * c:P * c + P], T.ta[:], start=True, stop=False)
+
+    ve.wait_ge(S.a2, n_in2)
+    for q in range(Q):
+        ve.tensor_tensor(T.tb[blk(q), blk(q)], T.m2[blk(q), 0:B], T.m2[blk(q), B:2 * B], AluOpType.add).then_inc(S.sb, 1)
+    pe.wait_ge(S.sb, Q)
+    for c in range(Q):
+        pe.matmul(T["py%d" % c][:, 0:P], T.z[:, P * c:P * c + P], T.tb[:], start=False, stop=True).then_inc(S["yd%d" % c], 1)
+    ve.wait_ge(S.x0, 16)
+    ve.wait_ge(S.x1, 16)
+    for c in range(Q):
+        ve.wait_ge(S["yd%d" % c], 1)
+        ve.tensor_tensor(T.ys[:, P * c:P * c + P], T.xs[:, P * c:P * c + P], T["py%d" % c][:, 0:P],
+                         AluOpType.subtract).then_inc(S["yo%d" % c], 1)
+    sy.wait_ge(S.yo0, 1)
+    sy.wait_ge(S.yo1, 1)
+    sy.dma_start(T.y[:, 0:H], T.ys[:, 0:H]).then_inc(S.s0, 16)
+    sc.wait_ge(S.yo2, 1)
+    sc.wait_ge(S.yo3, 1)
+    sc.dma_start(T.y[:, H:TK], T.ys[:, H:TK]).then_inc(S.s1, 16)
+    sy.wait_ge(S.s0, 16)
+    sc.wait_ge(S.s1, 16)
+    g.wait_ge(S.snt, sent)

@@ -6,26 +6,30 @@ TK = 512
 R = 8
 Q = 4
 B = 32
-WZ = B - R
+HB = B // 2
 
 SCRATCH = {
     "xs": ("sbuf", [P, TK], "float32"),
     "ys": ("sbuf", [P, TK], "float32"),
     "vr": ("sbuf", [P, R], "float32"),
-    "w": ("sbuf", [P, WZ + R + WZ], "float32"),
+    "v2": ("sbuf", [P, R], "float32"),
     "z": ("sbuf", [P, Q * P], "float32"),
     "own": ("sbuf", [P, B], "float32"),
     "l1": ("sbuf", [P, B], "float32"),
     "m2": ("sbuf", [P, 2 * B], "float32"),
+    "u": ("sbuf", [P, B], "float32"),
+    "sm": ("sbuf", [P, B], "float32"),
     "ta": ("sbuf", [P, P], "float32"),
     "tb": ("sbuf", [P, P], "float32"),
+    "pt0": ("psum", [P, TK], "float32"),
+    "pt1": ("psum", [P, TK], "float32"),
 }
 for _i in range(Q):
-    SCRATCH["pp%d" % _i] = ("psum", [P, TK], "float32")
     SCRATCH["py%d" % _i] = ("psum", [P, TK], "float32")
 
-SEMAPHORES = (["x0", "x1", "vl", "wz", "zz", "tz", "zl", "own", "a1", "a2", "snt", "sa", "sb", "s0", "s1"]
-              + ["pd%d" % i for i in range(Q)] + ["yd%d" % i for i in range(Q)] + ["yo%d" % i for i in range(Q)])
+SEMAPHORES = (["x0", "x1", "vl", "wz", "zz", "tz", "zl", "pd0", "pd1", "ow0", "ow1", "a10", "a11", "a2", "snt",
+               "su", "sa", "ss", "sb"]
+              + ["yd%d" % i for i in range(Q)] + ["yo%d" % i for i in range(Q)] + ["st%d" % i for i in range(Q)])
 
 
 def _links(topo, a, b):
@@ -93,51 +97,50 @@ def rank_program(g, core, T, topo):
     pe, ve, sy, sc = g.tensor, g.vector, g.sync, g.scalar
     H = TK // 2
 
-    def blk(q):
-        return slice(B * q, B * q + B)
+    def blk(a):
+        return slice(B * a, B * a + B)
+
+    def col(c):
+        return slice(P * c, P * c + P)
 
     sy.dma_start(T.xs[:, 0:H], T.x[:, 0:H]).then_inc(S.x0, 16)
     sc.dma_start(T.vr[:], T.v[:]).then_inc(S.vl, 16)
     sc.dma_start(T.xs[:, H:TK], T.x[:, H:TK]).then_inc(S.x1, 16)
 
-    ve.memset(T.w[:, 0:WZ], 0.0).then_inc(S.wz, 1)
-    ve.memset(T.w[:, WZ + R:WZ + R + WZ], 0.0).then_inc(S.wz, 1)
     ve.memset(T.z[:], 0.0).then_inc(S.zz, 1)
     ve.memset(T.ta[:], 0.0).then_inc(S.tz, 1)
     ve.memset(T.tb[:], 0.0).then_inc(S.tz, 1)
     ve.wait_ge(S.vl, 16)
-    ve.tensor_tensor(T.w[:, WZ:WZ + R], T.vr[:], T.vr[:], AluOpType.add).then_inc(S.wz, 1)
+    ve.tensor_tensor(T.v2[:], T.vr[:], T.vr[:], AluOpType.add).then_inc(S.wz, 1)
 
     sy.wait_ge(S.zz, 1)
     sc.wait_ge(S.zz, 1)
-    for q in range(Q):
+    for a in range(Q):
         for c in range(Q):
-            dq = sy if (q * Q + c) % 2 == 0 else sc
-            p0 = B * q + R * c
-            dq.dma_start(T.z[p0:p0 + R, P * c:P * c + P], T.vt[:]).then_inc(S.zl, 16)
+            dq = sy if (a * Q + c) % 2 == 0 else sc
+            p0 = B * a + R * c
+            dq.dma_start(T.z[p0:p0 + R, col(c)], T.vt[:]).then_inc(S.zl, 16)
 
-    pe.wait_ge(S.wz, 3)
-    pe.wait_ge(S.x0, 16)
-    for c in range(Q):
-        if c == Q // 2:
-            pe.wait_ge(S.x1, 16)
-        for q in range(Q):
-            col = (Q * c + q) * B
-            mm = pe.matmul(T["pp%d" % q][blk(q), 0:B], T.w[:, WZ - R * c:WZ - R * c + B], T.xs[:, col:col + B],
-                           start=(c == 0), stop=(c == Q - 1))
-            if c == Q - 1:
-                mm.then_inc(S["pd%d" % q], 1)
+    pe.wait_ge(S.wz, 1)
+    for h in range(2):
+        pe.wait_ge(S["x%d" % h], 16)
+        for e in range(2):
+            mm = pe.matmul(T["pt%d" % h][:, R * e:R * e + R], T.xs[:, col(2 * h + e)], T.v2[:], start=True, stop=True)
+        mm.then_inc(S["pd%d" % h], 1)
 
-    for q in range(Q):
-        ve.wait_ge(S["pd%d" % q], 1)
-        ve.tensor_copy(T.own[blk(q), :], T["pp%d" % q][blk(q), 0:B]).then_inc(S.own, 1)
+    for h in range(2):
+        ve.wait_ge(S["pd%d" % h], 1)
+        ve.tensor_copy(T.own[:, HB * h:HB * h + HB], T["pt%d" % h][:, 0:HB]).then_inc(S["ow%d" % h], 1)
 
     pc = cores[partner[rank]]
     m1 = topo.mask(core, pc)
     rid, pid = topo.addr(pc, core)
-    g.wait_ge(S.own, Q)
-    g.remote_dma(out_ap=T.l1[:], in_ap=T.own[:], remote_sem=S.a1, local_sem=S.snt, pid=pid, routing_id=rid,
-                 dma_engine_mask=m1)
+    sent = 0
+    for h in range(2):
+        g.wait_ge(S["ow%d" % h], 1)
+        g.remote_dma(out_ap=T.l1[:, HB * h:HB * h + HB], in_ap=T.own[:, HB * h:HB * h + HB], remote_sem=S["a1%d" % h],
+                     local_sem=S.snt, pid=pid, routing_id=rid, dma_engine_mask=m1)
+        sent += _count(m1)
     n_in1 = _count(topo.mask(pc, core))
 
     def slot(dst, src):
@@ -149,8 +152,8 @@ def rank_program(g, core, T, topo):
             m &= topo.mask(cores[src], cores[d])
         return m
 
-    g.wait_ge(S.a1, n_in1)
-    sent = _count(m1)
+    g.wait_ge(S.a10, n_in1)
+    g.wait_ge(S.a11, n_in1)
     if dests[rank]:
         ids, aps = [], []
         for d in dests[rank]:
@@ -163,34 +166,39 @@ def rank_program(g, core, T, topo):
         sent += _count(mask2(rank))
     n_in2 = sum(_count(mask2(s)) for s in range(len(cores)) if rank in dests[s])
 
-    ve.wait_ge(S.own, Q)
+    ve.wait_ge(S.ow0, 1)
+    ve.wait_ge(S.ow1, 1)
     ve.wait_ge(S.tz, 2)
-    ve.wait_ge(S.a1, n_in1)
-    for q in range(Q):
-        ve.tensor_tensor(T.ta[blk(q), blk(q)], T.own[blk(q), :], T.l1[blk(q), :], AluOpType.add).then_inc(S.sa, 1)
+    ve.wait_ge(S.a10, n_in1)
+    ve.wait_ge(S.a11, n_in1)
+    ve.tensor_tensor(T.u[:], T.own[:], T.l1[:], AluOpType.add).then_inc(S.su, 1)
+    ve.wait_ge(S.su, 1)
+    for a in range(Q):
+        ve.transpose(T.ta[blk(a), blk(a)], T.u[blk(a), :]).then_inc(S.sa, 1)
     pe.wait_ge(S.zl, 16 * Q * Q)
     pe.wait_ge(S.sa, Q)
     for c in range(Q):
-        pe.matmul(T["py%d" % c][:, 0:P], T.z[:, P * c:P * c + P], T.ta[:], start=True, stop=False)
+        pe.matmul(T["py%d" % c][:, 0:P], T.z[:, col(c)], T.ta[:], start=True, stop=False)
 
     ve.wait_ge(S.a2, n_in2)
-    for q in range(Q):
-        ve.tensor_tensor(T.tb[blk(q), blk(q)], T.m2[blk(q), 0:B], T.m2[blk(q), B:2 * B], AluOpType.add).then_inc(S.sb, 1)
+    ve.tensor_tensor(T.sm[:], T.m2[:, 0:B], T.m2[:, B:2 * B], AluOpType.add).then_inc(S.ss, 1)
+    ve.wait_ge(S.ss, 1)
+    for a in range(Q):
+        ve.transpose(T.tb[blk(a), blk(a)], T.sm[blk(a), :]).then_inc(S.sb, 1)
     pe.wait_ge(S.sb, Q)
     for c in range(Q):
-        pe.matmul(T["py%d" % c][:, 0:P], T.z[:, P * c:P * c + P], T.tb[:], start=False, stop=True).then_inc(S["yd%d" % c], 1)
+        pe.matmul(T["py%d" % c][:, 0:P], T.z[:, col(c)], T.tb[:], start=False, stop=True).then_inc(S["yd%d" % c], 1)
     ve.wait_ge(S.x0, 16)
     ve.wait_ge(S.x1, 16)
     for c in range(Q):
         ve.wait_ge(S["yd%d" % c], 1)
-        ve.tensor_tensor(T.ys[:, P * c:P * c + P], T.xs[:, P * c:P * c + P], T["py%d" % c][:, 0:P],
+        ve.tensor_tensor(T.ys[:, col(c)], T.xs[:, col(c)], T["py%d" % c][:, 0:P],
                          AluOpType.subtract).then_inc(S["yo%d" % c], 1)
-    sy.wait_ge(S.yo0, 1)
-    sy.wait_ge(S.yo1, 1)
-    sy.dma_start(T.y[:, 0:H], T.ys[:, 0:H]).then_inc(S.s0, 16)
-    sc.wait_ge(S.yo2, 1)
-    sc.wait_ge(S.yo3, 1)
-    sc.dma_start(T.y[:, H:TK], T.ys[:, H:TK]).then_inc(S.s1, 16)
-    sy.wait_ge(S.s0, 16)
-    sc.wait_ge(S.s1, 16)
+    for c in range(Q):
+        dq = sy if c % 2 == 0 else sc
+        dq.wait_ge(S["yo%d" % c], 1)
+        dq.dma_start(T.y[:, col(c)], T.ys[:, col(c)]).then_inc(S["st%d" % c], 16)
+    for c in range(Q):
+        dq = sy if c % 2 == 0 else sc
+        dq.wait_ge(S["st%d" % c], 16)
     g.wait_ge(S.snt, sent)

@@ -1,35 +1,35 @@
 from concourse.bass import DstId, RemoteDMATransfer
-from concourse.mybir import AluOpType
+from concourse.mybir import AluOpType, ActivationFunctionType
 
 P = 128
 TK = 512
 R = 8
 Q = 4
 B = 32
-HB = B // 2
+HP = P // 2
+WW = P + B
 
 SCRATCH = {
     "xs": ("sbuf", [P, TK], "float32"),
     "ys": ("sbuf", [P, TK], "float32"),
     "vr": ("sbuf", [P, R], "float32"),
-    "v2": ("sbuf", [P, R], "float32"),
+    "vts": ("sbuf", [P, P], "float32"),
+    "w": ("sbuf", [P, WW], "float32"),
     "z": ("sbuf", [P, Q * P], "float32"),
     "own": ("sbuf", [P, B], "float32"),
     "l1": ("sbuf", [P, B], "float32"),
     "m2": ("sbuf", [P, 2 * B], "float32"),
-    "u": ("sbuf", [P, B], "float32"),
-    "sm": ("sbuf", [P, B], "float32"),
-    "ta": ("sbuf", [P, P], "float32"),
-    "tb": ("sbuf", [P, P], "float32"),
-    "pt0": ("psum", [P, TK], "float32"),
-    "pt1": ("psum", [P, TK], "float32"),
+    "r": ("sbuf", [P, P], "float32"),
+    "pta": ("psum", [P, TK], "float32"),
+    "ptb": ("psum", [P, TK], "float32"),
 }
-for _i in range(Q):
+for _i in range(Q + 1):
     SCRATCH["py%d" % _i] = ("psum", [P, TK], "float32")
 
-SEMAPHORES = (["x0", "x1", "vl", "wz", "zz", "tz", "zl", "pd0", "pd1", "ow0", "ow1", "a10", "a11", "a2", "snt",
-               "su", "sa", "ss", "sb"]
-              + ["yd%d" % i for i in range(Q)] + ["yo%d" % i for i in range(Q)] + ["st%d" % i for i in range(Q)])
+SEMAPHORES = (["xa", "xb", "xc", "vl", "vtl", "on", "wr", "pda", "pdb", "owa", "owb", "a10", "a11", "snt",
+               "se", "sl0", "sl1", "zc"]
+              + ["a2_%d" % i for i in range(6)] + ["zp%d" % i for i in range(Q)]
+              + ["yd%d" % i for i in range(Q + 1)] + ["yo%d" % i for i in range(Q + 1)] + ["st%d" % i for i in range(Q + 1)])
 
 
 def _links(topo, a, b):
@@ -83,6 +83,28 @@ def _plan(cores, topo):
     return best[1], best[2]
 
 
+def _balance(dests):
+    n = len(dests)
+    best = [None, None]
+
+    def go(s, chosen):
+        if s == n:
+            first = [0] * n
+            for d in chosen:
+                if d:
+                    first[d[0]] += 1
+            key = max(first)
+            if best[0] is None or key < best[0]:
+                best[0], best[1] = key, [list(d) for d in chosen]
+            return
+        d = dests[s]
+        for k in range(max(1, len(d))):
+            go(s + 1, chosen + [d[k:] + d[:k]])
+
+    go(0, [])
+    return best[1]
+
+
 def _count(mask):
     return bin(mask).count("1")
 
@@ -93,9 +115,9 @@ def rank_program(g, core, T, topo):
         return
     cores = list(T.cores)
     partner, dests = _plan(cores, topo)
+    dests = _balance(dests)
     S = T.sem
     pe, ve, sy, sc = g.tensor, g.vector, g.sync, g.scalar
-    H = TK // 2
 
     def blk(a):
         return slice(B * a, B * a + B)
@@ -103,48 +125,43 @@ def rank_program(g, core, T, topo):
     def col(c):
         return slice(P * c, P * c + P)
 
-    sy.dma_start(T.xs[:, 0:H], T.x[:, 0:H]).then_inc(S.x0, 16)
+    sy.dma_start(T.xs[:, 0:P], T.x[:, 0:P]).then_inc(S.xa, 16)
     sc.dma_start(T.vr[:], T.v[:]).then_inc(S.vl, 16)
-    sc.dma_start(T.xs[:, H:TK], T.x[:, H:TK]).then_inc(S.x1, 16)
+    sy.dma_start(T.xs[:, P:3 * P], T.x[:, P:3 * P]).then_inc(S.xb, 16)
+    sc.dma_start(T.vts[0:R, :], T.vt[:]).then_inc(S.vtl, 16)
+    sy.dma_start(T.xs[:, 3 * P:TK], T.x[:, 3 * P:TK]).then_inc(S.xc, 16)
 
-    ve.memset(T.z[:], 0.0).then_inc(S.zz, 1)
-    ve.memset(T.ta[:], 0.0).then_inc(S.tz, 1)
-    ve.memset(T.tb[:], 0.0).then_inc(S.tz, 1)
-    ve.wait_ge(S.vl, 16)
-    ve.tensor_tensor(T.v2[:], T.vr[:], T.vr[:], AluOpType.add).then_inc(S.wz, 1)
+    ve.memset(T.w[0:R, :], 1.0).then_inc(S.on, 1)
+    g.wait_ge(S.on, 1)
+    g.affine_select(T.w[0:R, :], T.w[0:R, :], [[0, WW // B], [1, B]], AluOpType.is_equal, 0.0, -(B - R), -1).then_inc(S.wr, 1)
 
-    sy.wait_ge(S.zz, 1)
-    sc.wait_ge(S.zz, 1)
-    for a in range(Q):
-        for c in range(Q):
-            dq = sy if (a * Q + c) % 2 == 0 else sc
-            p0 = B * a + R * c
-            dq.dma_start(T.z[p0:p0 + R, col(c)], T.vt[:]).then_inc(S.zl, 16)
+    pe.wait_ge(S.vl, 16)
+    pe.wait_ge(S.xa, 16)
+    pe.matmul(T.pta[:, 0:R], T.xs[:, col(0)], T.vr[:], start=True, stop=True).then_inc(S.pda, 1)
+    pe.wait_ge(S.xb, 16)
+    pe.matmul(T.ptb[:, 0:R], T.xs[:, col(1)], T.vr[:], start=True, stop=True)
+    pe.matmul(T.ptb[:, R:2 * R], T.xs[:, col(2)], T.vr[:], start=True, stop=True)
+    pe.wait_ge(S.xc, 16)
+    pe.matmul(T.ptb[:, 2 * R:3 * R], T.xs[:, col(3)], T.vr[:], start=True, stop=True).then_inc(S.pdb, 1)
 
-    pe.wait_ge(S.wz, 1)
-    for h in range(2):
-        pe.wait_ge(S["x%d" % h], 16)
-        for e in range(2):
-            mm = pe.matmul(T["pt%d" % h][:, R * e:R * e + R], T.xs[:, col(2 * h + e)], T.v2[:], start=True, stop=True)
-        mm.then_inc(S["pd%d" % h], 1)
-
-    for h in range(2):
-        ve.wait_ge(S["pd%d" % h], 1)
-        ve.tensor_copy(T.own[:, HB * h:HB * h + HB], T["pt%d" % h][:, 0:HB]).then_inc(S["ow%d" % h], 1)
+    ve.wait_ge(S.pda, 1)
+    ve.tensor_copy(T.own[:, 0:R], T.pta[:, 0:R]).then_inc(S.owa, 1)
+    ve.wait_ge(S.pdb, 1)
+    ve.tensor_copy(T.own[:, R:B], T.ptb[:, 0:B - R]).then_inc(S.owb, 1)
 
     pc = cores[partner[rank]]
     m1 = topo.mask(core, pc)
     rid, pid = topo.addr(pc, core)
     sent = 0
-    for h in range(2):
-        g.wait_ge(S["ow%d" % h], 1)
-        g.remote_dma(out_ap=T.l1[:, HB * h:HB * h + HB], in_ap=T.own[:, HB * h:HB * h + HB], remote_sem=S["a1%d" % h],
+    for lo, hi, ow, ar in ((0, R, S.owa, S.a10), (R, B, S.owb, S.a11)):
+        g.wait_ge(ow, 1)
+        g.remote_dma(out_ap=T.l1[:, lo:hi], in_ap=T.own[:, lo:hi], remote_sem=ar,
                      local_sem=S.snt, pid=pid, routing_id=rid, dma_engine_mask=m1)
         sent += _count(m1)
     n_in1 = _count(topo.mask(pc, core))
 
-    def slot(dst, src):
-        return sorted(s for s in range(len(cores)) if dst in dests[s]).index(src)
+    def senders(dst):
+        return sorted((s for s in range(len(cores)) if dst in dests[s]), key=lambda s: (dests[s].index(dst), s))
 
     def mask2(src):
         m = -1
@@ -159,46 +176,61 @@ def rank_program(g, core, T, topo):
         for d in dests[rank]:
             rid, pid = topo.addr(cores[d], core)
             ids.append(DstId(rid=rid, pnc=pid))
-            k = slot(d, rank)
+            k = senders(d).index(rank)
             aps.append(T.m2[:, B * k:B * k + B])
-        g.remote_dma_fused([RemoteDMATransfer(dst_ids=ids, dma_engine_mask=mask2(rank), remote_sem=S.a2,
+        g.remote_dma_fused([RemoteDMATransfer(dst_ids=ids, dma_engine_mask=mask2(rank), remote_sem=S["a2_%d" % rank],
                                               srcs=[T.own[:], T.l1[:]], dsts=aps, alu_op=1)], local_sem=S.snt)
         sent += _count(mask2(rank))
-    n_in2 = sum(_count(mask2(s)) for s in range(len(cores)) if rank in dests[s])
 
-    ve.wait_ge(S.ow0, 1)
-    ve.wait_ge(S.ow1, 1)
-    ve.wait_ge(S.tz, 2)
+    pe.wait_ge(S.wr, 1)
+    pe.wait_ge(S.vtl, 16)
+    for c in range(Q):
+        u = B - R - R * c
+        pe.matmul(T["py%d" % c][:, 0:P], T.w[0:R, u:u + P], T.vts[0:R, :], start=True, stop=True).then_inc(S["zp%d" % c], 1)
+    for c in range(Q):
+        sc.wait_ge(S["zp%d" % c], 1)
+        sc.activation(T.z[:, col(c)], T["py%d" % c][:, 0:P], ActivationFunctionType.Copy, scale=2.0).then_inc(S.zc, 1)
+
+    ve.wait_ge(S.owa, 1)
+    ve.wait_ge(S.owb, 1)
+    for a in range(Q):
+        ve.transpose(T.r[blk(0), blk(a)], T.own[blk(a), :]).then_inc(S.se, 1)
     ve.wait_ge(S.a10, n_in1)
     ve.wait_ge(S.a11, n_in1)
-    ve.tensor_tensor(T.u[:], T.own[:], T.l1[:], AluOpType.add).then_inc(S.su, 1)
-    ve.wait_ge(S.su, 1)
     for a in range(Q):
-        ve.transpose(T.ta[blk(a), blk(a)], T.u[blk(a), :]).then_inc(S.sa, 1)
-    pe.wait_ge(S.zl, 16 * Q * Q)
-    pe.wait_ge(S.sa, Q)
-    for c in range(Q):
-        pe.matmul(T["py%d" % c][:, 0:P], T.z[:, col(c)], T.ta[:], start=True, stop=False)
+        ve.transpose(T.r[blk(1), blk(a)], T.l1[blk(a), :]).then_inc(S.se, 1)
+    s_first, s_last = senders(rank)
+    ve.wait_ge(S["a2_%d" % s_first], _count(mask2(s_first)))
+    for a in range(Q):
+        ve.transpose(T.r[blk(2), blk(a)], T.m2[blk(a), 0:B]).then_inc(S.se, 1)
+    ve.wait_ge(S["a2_%d" % s_last], _count(mask2(s_last)))
+    for a in range(Q):
+        ve.transpose(T.r[blk(3), blk(a)], T.m2[blk(a), B:2 * B]).then_inc(S.sl0 if a < Q // 2 else S.sl1, 1)
 
-    ve.wait_ge(S.a2, n_in2)
-    ve.tensor_tensor(T.sm[:], T.m2[:, 0:B], T.m2[:, B:2 * B], AluOpType.add).then_inc(S.ss, 1)
-    ve.wait_ge(S.ss, 1)
-    for a in range(Q):
-        ve.transpose(T.tb[blk(a), blk(a)], T.sm[blk(a), :]).then_inc(S.sb, 1)
-    pe.wait_ge(S.sb, Q)
-    for c in range(Q):
-        pe.matmul(T["py%d" % c][:, 0:P], T.z[:, col(c)], T.tb[:], start=False, stop=True).then_inc(S["yd%d" % c], 1)
-    ve.wait_ge(S.x0, 16)
-    ve.wait_ge(S.x1, 16)
-    for c in range(Q):
-        ve.wait_ge(S["yd%d" % c], 1)
-        ve.tensor_tensor(T.ys[:, col(c)], T.xs[:, col(c)], T["py%d" % c][:, 0:P],
-                         AluOpType.subtract).then_inc(S["yo%d" % c], 1)
-    for c in range(Q):
-        dq = sy if c % 2 == 0 else sc
-        dq.wait_ge(S["yo%d" % c], 1)
-        dq.dma_start(T.y[:, col(c)], T.ys[:, col(c)]).then_inc(S["st%d" % c], 16)
-    for c in range(Q):
-        dq = sy if c % 2 == 0 else sc
-        dq.wait_ge(S["st%d" % c], 16)
+    pe.wait_ge(S.zc, Q)
+    pe.wait_ge(S.se, 3 * Q)
+    pe.wait_ge(S.sl0, Q // 2)
+    pe.matmul(T.py0[:, 0:HP], T.z[:, col(0)], T.r[:, 0:HP], start=True, stop=True)
+    pe.wait_ge(S.sl1, Q // 2)
+    pe.matmul(T.py0[:, HP:P], T.z[:, col(0)], T.r[:, HP:P], start=True, stop=True).then_inc(S.yd0, 1)
+    pe.matmul(T.py1[:, 0:P], T.z[:, col(1)], T.r[:], start=True, stop=True).then_inc(S.yd1, 1)
+    pe.matmul(T.py2[:, 0:P], T.z[:, col(2)], T.r[:], start=True, stop=True).then_inc(S.yd2, 1)
+    pe.matmul(T.py3[:, 0:HP], T.z[:, col(3)], T.r[:, 0:HP], start=True, stop=True).then_inc(S.yd3, 1)
+    pe.matmul(T.py4[:, 0:HP], T.z[:, col(3)], T.r[:, HP:P], start=True, stop=True).then_inc(S.yd4, 1)
+
+    pieces = [(0, P), (P, P), (2 * P, P), (3 * P, HP), (3 * P + HP, HP)]
+    ve.wait_ge(S.xa, 16)
+    ve.wait_ge(S.xb, 16)
+    ve.wait_ge(S.xc, 16)
+    for i, (lo, n) in enumerate(pieces):
+        ve.wait_ge(S["yd%d" % i], 1)
+        ve.tensor_tensor(T.ys[:, lo:lo + n], T.xs[:, lo:lo + n], T["py%d" % i][:, 0:n],
+                         AluOpType.subtract).then_inc(S["yo%d" % i], 1)
+    for i, (lo, n) in enumerate(pieces):
+        dq = sy if i % 2 == 0 else sc
+        dq.wait_ge(S["yo%d" % i], 1)
+        dq.dma_start(T.y[:, lo:lo + n], T.ys[:, lo:lo + n]).then_inc(S["st%d" % i], 16)
+    for i in range(len(pieces)):
+        dq = sy if i % 2 == 0 else sc
+        dq.wait_ge(S["st%d" % i], 16)
     g.wait_ge(S.snt, sent)

from concourse.bass import DstId, RemoteDMATransfer
from concourse.mybir import AluOpType, ActivationFunctionType

P = 128
TK = 512
R = 8
Q = 4
B = 32
HP = P // 2
WW = P + B

SCRATCH = {
    "xs": ("sbuf", [P, TK], "float32"),
    "ys": ("sbuf", [P, TK], "float32"),
    "vr": ("sbuf", [P, R], "float32"),
    "vts": ("sbuf", [P, P], "float32"),
    "w": ("sbuf", [P, WW], "float32"),
    "z": ("sbuf", [P, Q * P], "float32"),
    "own": ("sbuf", [P, B], "float32"),
    "l1": ("sbuf", [P, B], "float32"),
    "m2": ("sbuf", [P, 2 * B], "float32"),
    "r": ("sbuf", [P, P], "float32"),
    "pta": ("psum", [P, TK], "float32"),
    "ptb": ("psum", [P, TK], "float32"),
}
for _i in range(Q + 1):
    SCRATCH["py%d" % _i] = ("psum", [P, TK], "float32")

SEMAPHORES = (["xa", "xb", "xc", "vl", "vtl", "on", "wr", "pda", "pdb", "owa", "owb", "a10", "a11", "snt",
               "se", "sl0", "sl1", "zc"]
              + ["a2_%d" % i for i in range(6)] + ["zp%d" % i for i in range(Q)]
              + ["yd%d" % i for i in range(Q + 1)] + ["yo%d" % i for i in range(Q + 1)] + ["st%d" % i for i in range(Q + 1)])


def _links(topo, a, b):
    if topo.host(a) == topo.host(b) and topo.chip(a) == topo.chip(b):
        return 0
    if topo.rack(topo.host(a)) == topo.rack(topo.host(b)):
        return 1 if (topo.mates(a, b) or topo.same_plane(a, b)) else 2
    return 1 if topo.chip(a) == topo.chip(b) else 3


def _pairings(items):
    if not items:
        return [[]]
    out = []
    for i in range(1, len(items)):
        for m in _pairings(items[1:i] + items[i + 1:]):
            out.append([(items[0], items[i])] + m)
    return out


def _plan(cores, topo):
    n = len(cores)
    best = None
    for m in _pairings(list(range(n))):
        if not all(topo.may_write(cores[a], cores[b]) and topo.may_write(cores[b], cores[a]) for a, b in m):
            continue
        cost = sum(2 * _links(topo, cores[a], cores[b]) for a, b in m)
        dests = [[] for _ in range(n)]
        ok = True
        for r in range(n):
            for pair in m:
                if r in pair:
                    continue
                cand = [s for s in pair if topo.may_write(cores[s], cores[r])]
                if not cand:
                    ok = False
                    break
                s = min(cand, key=lambda s: (_links(topo, cores[s], cores[r]), len(dests[s]), s))
                dests[s].append(r)
                cost += _links(topo, cores[s], cores[r])
            if not ok:
                break
        if not ok:
            continue
        key = (max(len(d) for d in dests), cost)
        if best is None or key < best[0]:
            partner = [0] * n
            for a, b in m:
                partner[a], partner[b] = b, a
            best = (key, partner, dests)
    return best[1], best[2]


def _balance(dests):
    n = len(dests)
    best = [None, None]

    def go(s, chosen):
        if s == n:
            first = [0] * n
            for d in chosen:
                if d:
                    first[d[0]] += 1
            key = max(first)
            if best[0] is None or key < best[0]:
                best[0], best[1] = key, [list(d) for d in chosen]
            return
        d = dests[s]
        for k in range(max(1, len(d))):
            go(s + 1, chosen + [d[k:] + d[:k]])

    go(0, [])
    return best[1]


def _count(mask):
    return bin(mask).count("1")


def rank_program(g, core, T, topo):
    rank = T.rank_of(core)
    if rank is None:
        return
    cores = list(T.cores)
    partner, dests = _plan(cores, topo)
    dests = _balance(dests)
    S = T.sem
    pe, ve, sy, sc = g.tensor, g.vector, g.sync, g.scalar

    def blk(a):
        return slice(B * a, B * a + B)

    def col(c):
        return slice(P * c, P * c + P)

    sy.dma_start(T.xs[:, 0:P], T.x[:, 0:P]).then_inc(S.xa, 16)
    sc.dma_start(T.vr[:], T.v[:]).then_inc(S.vl, 16)
    sy.dma_start(T.xs[:, P:3 * P], T.x[:, P:3 * P]).then_inc(S.xb, 16)
    sc.dma_start(T.vts[0:R, :], T.vt[:]).then_inc(S.vtl, 16)
    sy.dma_start(T.xs[:, 3 * P:TK], T.x[:, 3 * P:TK]).then_inc(S.xc, 16)

    ve.memset(T.w[0:R, :], 1.0).then_inc(S.on, 1)
    g.wait_ge(S.on, 1)
    g.affine_select(T.w[0:R, :], T.w[0:R, :], [[0, WW // B], [1, B]], AluOpType.is_equal, 0.0, -(B - R), -1).then_inc(S.wr, 1)

    pe.wait_ge(S.vl, 16)
    pe.wait_ge(S.xa, 16)
    pe.matmul(T.pta[:, 0:R], T.xs[:, col(0)], T.vr[:], start=True, stop=True).then_inc(S.pda, 1)
    pe.wait_ge(S.xb, 16)
    pe.matmul(T.ptb[:, 0:R], T.xs[:, col(1)], T.vr[:], start=True, stop=True)
    pe.matmul(T.ptb[:, R:2 * R], T.xs[:, col(2)], T.vr[:], start=True, stop=True)
    pe.wait_ge(S.xc, 16)
    pe.matmul(T.ptb[:, 2 * R:3 * R], T.xs[:, col(3)], T.vr[:], start=True, stop=True).then_inc(S.pdb, 1)

    ve.wait_ge(S.pda, 1)
    ve.tensor_copy(T.own[:, 0:R], T.pta[:, 0:R]).then_inc(S.owa, 1)
    ve.wait_ge(S.pdb, 1)
    ve.tensor_copy(T.own[:, R:B], T.ptb[:, 0:B - R]).then_inc(S.owb, 1)

    pc = cores[partner[rank]]
    m1 = topo.mask(core, pc)
    rid, pid = topo.addr(pc, core)
    sent = 0
    for lo, hi, ow, ar in ((0, R, S.owa, S.a10), (R, B, S.owb, S.a11)):
        g.wait_ge(ow, 1)
        g.remote_dma(out_ap=T.l1[:, lo:hi], in_ap=T.own[:, lo:hi], remote_sem=ar,
                     local_sem=S.snt, pid=pid, routing_id=rid, dma_engine_mask=m1)
        sent += _count(m1)
    n_in1 = _count(topo.mask(pc, core))

    def senders(dst):
        return sorted((s for s in range(len(cores)) if dst in dests[s]), key=lambda s: (dests[s].index(dst), s))

    def mask2(src):
        m = -1
        for d in dests[src]:
            m &= topo.mask(cores[src], cores[d])
        return m

    g.wait_ge(S.a10, n_in1)
    g.wait_ge(S.a11, n_in1)
    if dests[rank]:
        ids, aps = [], []
        for d in dests[rank]:
            rid, pid = topo.addr(cores[d], core)
            ids.append(DstId(rid=rid, pnc=pid))
            k = senders(d).index(rank)
            aps.append(T.m2[:, B * k:B * k + B])
        g.remote_dma_fused([RemoteDMATransfer(dst_ids=ids, dma_engine_mask=mask2(rank), remote_sem=S["a2_%d" % rank],
                                              srcs=[T.own[:], T.l1[:]], dsts=aps, alu_op=1)], local_sem=S.snt)
        sent += _count(mask2(rank))

    pe.wait_ge(S.wr, 1)
    pe.wait_ge(S.vtl, 16)
    for c in range(Q):
        u = B - R - R * c
        pe.matmul(T["py%d" % c][:, 0:P], T.w[0:R, u:u + P], T.vts[0:R, :], start=True, stop=True).then_inc(S["zp%d" % c], 1)
    for c in range(Q):
        sc.wait_ge(S["zp%d" % c], 1)
        sc.activation(T.z[:, col(c)], T["py%d" % c][:, 0:P], ActivationFunctionType.Copy, scale=2.0).then_inc(S.zc, 1)

    ve.wait_ge(S.owa, 1)
    ve.wait_ge(S.owb, 1)
    for a in range(Q):
        ve.transpose(T.r[blk(0), blk(a)], T.own[blk(a), :]).then_inc(S.se, 1)
    ve.wait_ge(S.a10, n_in1)
    ve.wait_ge(S.a11, n_in1)
    for a in range(Q):
        ve.transpose(T.r[blk(1), blk(a)], T.l1[blk(a), :]).then_inc(S.se, 1)
    s_first, s_last = senders(rank)
    ve.wait_ge(S["a2_%d" % s_first], _count(mask2(s_first)))
    for a in range(Q):
        ve.transpose(T.r[blk(2), blk(a)], T.m2[blk(a), 0:B]).then_inc(S.se, 1)
    ve.wait_ge(S["a2_%d" % s_last], _count(mask2(s_last)))
    for a in range(Q):
        ve.transpose(T.r[blk(3), blk(a)], T.m2[blk(a), B:2 * B]).then_inc(S.sl0 if a < Q // 2 else S.sl1, 1)

    pe.wait_ge(S.zc, Q)
    pe.wait_ge(S.se, 3 * Q)
    pe.wait_ge(S.sl0, Q // 2)
    pe.matmul(T.py0[:, 0:HP], T.z[:, col(0)], T.r[:, 0:HP], start=True, stop=True)
    pe.wait_ge(S.sl1, Q // 2)
    pe.matmul(T.py0[:, HP:P], T.z[:, col(0)], T.r[:, HP:P], start=True, stop=True).then_inc(S.yd0, 1)
    pe.matmul(T.py1[:, 0:P], T.z[:, col(1)], T.r[:], start=True, stop=True).then_inc(S.yd1, 1)
    pe.matmul(T.py2[:, 0:P], T.z[:, col(2)], T.r[:], start=True, stop=True).then_inc(S.yd2, 1)
    pe.matmul(T.py3[:, 0:HP], T.z[:, col(3)], T.r[:, 0:HP], start=True, stop=True).then_inc(S.yd3, 1)
    pe.matmul(T.py4[:, 0:HP], T.z[:, col(3)], T.r[:, HP:P], start=True, stop=True).then_inc(S.yd4, 1)

    pieces = [(0, P), (P, P), (2 * P, P), (3 * P, HP), (3 * P + HP, HP)]
    ve.wait_ge(S.xa, 16)
    ve.wait_ge(S.xb, 16)
    ve.wait_ge(S.xc, 16)
    for i, (lo, n) in enumerate(pieces):
        ve.wait_ge(S["yd%d" % i], 1)
        ve.tensor_tensor(T.ys[:, lo:lo + n], T.xs[:, lo:lo + n], T["py%d" % i][:, 0:n],
                         AluOpType.subtract).then_inc(S["yo%d" % i], 1)
    for i, (lo, n) in enumerate(pieces):
        dq = sy if i % 2 == 0 else sc
        dq.wait_ge(S["yo%d" % i], 1)
        dq.dma_start(T.y[:, lo:lo + n], T.ys[:, lo:lo + n]).then_inc(S["st%d" % i], 16)
    for i in range(len(pieces)):
        dq = sy if i % 2 == 0 else sc
        dq.wait_ge(S["st%d" % i], 16)
    g.wait_ge(S.snt, sent)
